import numpy as np
import ml_dtypes


def mxq(x, axis, fmt="e4m3"):
    dtype, down = {"e4m3": (ml_dtypes.float8_e4m3fn, 7), "e5m2": (ml_dtypes.float8_e5m2, 14)}[fmt]
    v = np.moveaxis(np.asarray(x, np.float32).astype(ml_dtypes.bfloat16).astype(np.float64), axis, -1)
    blocks = v.reshape(v.shape[:-1] + (-1, 32))
    amax = np.abs(blocks).max(-1, keepdims=True)
    byte = np.maximum(np.where(amax > 0, np.frexp(amax)[1] - 1 + 127, 0) - down, 1)
    scale = np.exp2(byte - 127.0)
    codes = (blocks / scale).astype(np.float32).astype(dtype).astype(np.float64)
    return np.moveaxis((codes * scale).reshape(v.shape), -1, axis)


WIDE = False


def mx_kscale(k):
    if not WIDE:
        return np.ones(k)
    levels = np.array([30, -30])
    if k % 512:
        return np.exp2(np.random.permutation(np.resize(levels, k // 32))).repeat(32)
    a = np.empty((k // 512, 16))
    for p in range(k // 512):
        a[p, :8] = np.random.permutation(np.resize(levels, 8))
        for g in range(8):
            far = levels[np.abs(levels - a[p, g]) >= 10]
            a[p, g + 8] = far[np.random.randint(len(far))]
    return np.exp2(a.ravel()).repeat(32)


def f64(x):
    return np.asarray(x).astype(np.float64)


def striped(idx):
    return np.tile(np.asarray(idx).reshape(-1, 16).T, (8, 1)).astype(np.uint16)


def unstriped(offs):
    return offs[:16].T.reshape(-1).astype(np.int64)


E2M1 = np.array([0.0, 0.5, 1.0, 1.5, 2.0, 3.0, 4.0, 6.0, -0.0, -0.5, -1.0, -1.5, -2.0, -3.0, -4.0, -6.0])


def pack_weight(w, fmt):
    k, n = w.shape
    w = f64(np.asarray(w, np.float32).astype(ml_dtypes.bfloat16)).reshape(k // 32, 32, n)
    amax = np.abs(w).max(1)
    if fmt == "e4m3":
        byte = np.frexp(amax)[1] - 1 + 127 - 7
    else:
        mant, ex = np.frexp(amax / 6.0)
        byte = np.where(mant > 0.5, ex, ex - 1) + 127
    byte = np.clip(np.where(amax > 0, byte, 1), 1, 254)
    scaled = (w * np.exp2(127.0 - byte)[:, None, :]).reshape(k, n).astype(np.float32)
    by_word = np.ascontiguousarray(scaled.reshape(k // 512, 128, 4, n).transpose(0, 1, 3, 2))
    if fmt == "e4m3":
        words = by_word.astype(ml_dtypes.float8_e4m3fn).view(np.uint8)
    else:
        c = by_word.astype(ml_dtypes.float4_e2m1fn).view(np.uint8) & 0xF
        words = (c[..., 0::2] | (c[..., 1::2] << 4)).reshape(k // 512, 128, 2 * n)
    return np.ascontiguousarray(words), np.ascontiguousarray(byte.astype(np.uint8).reshape(k // 512, 16, n))


def unpack_weight(words, scales, fmt):
    g, _, n = scales.shape
    words = np.ascontiguousarray(words).reshape(g, 128, n, -1)
    if fmt == "e4m3":
        vals = words.view(ml_dtypes.float8_e4m3fn).astype(np.float64)
    else:
        nib = np.empty((g, 128, n, 4), np.uint8)
        nib[..., 0::2] = words & 0xF
        nib[..., 1::2] = words >> 4
        vals = E2M1[nib]
    vals = vals * np.repeat(np.exp2(scales.astype(np.float64) - 127.0), 8, axis=1)[..., None]
    return vals.transpose(0, 1, 3, 2).reshape(g * 512, n)


def sigmoid(v):
    return 1.0 / (1.0 + np.exp(-v))


def sgn(shape):
    return np.random.uniform(0.5, 2.0, shape) * np.where(np.random.standard_normal(shape) < 0, -1.0, 1.0)


K, T, J, R, F, Z, O, N, E = 512, 1024, 256, 512, 512, 1024, 128, 256, 1024


def setup_inputs():
    n = np.random.standard_normal
    idx = np.random.permutation(T)[:J]
    idx2 = np.random.permutation(Z)[:J]
    idx3 = np.random.permutation(J)[:O]
    idx4 = np.random.permutation(J)[:O]
    idx5 = np.random.permutation(J)[:O]
    idx6 = np.random.permutation(T)[:O]
    idx7 = np.random.permutation(E)[:O]
    fk = mx_kscale(K)
    ff = mx_kscale(F)
    fr = mx_kscale(R)
    xtp = pack_weight(n((K, T)) / fk[:, None], "e2m1")
    xop = pack_weight(n((F, Z)) / ff[:, None], "e4m3")
    wp = pack_weight(n((K, R)) * 1 / np.sqrt(K) * fk[:, None], "e4m3")
    w2p = pack_weight(n((F, R)) * 1 / np.sqrt(F) * ff[:, None], "e2m1")
    wbp = pack_weight(n((R, N)) * 1 / np.sqrt(R) / fr[:, None], "e2m1")
    wsp = pack_weight(n((K, N)) * 1 / np.sqrt(K) * fk[:, None], "e4m3")
    return {
        "xt_words": xtp[0],
        "xt_scales": xtp[1],
        "xo_words": xop[0],
        "xo_scales": xop[1],
        "w_words": wp[0],
        "w_scales": wp[1],
        "w2_words": w2p[0],
        "w2_scales": w2p[1],
        "sa": (np.random.uniform(0.5, 1.6, (R, 1)) * fr[:, None]).astype(np.float32),
        "sb": (np.random.uniform(0.5, 1.6, (R, 1)) * fr[:, None]).astype(np.float32),
        "sg": (sgn((R, 1))).astype(np.float32),
        "wb_words": wbp[0],
        "wb_scales": wbp[1],
        "ws_words": wsp[0],
        "ws_scales": wsp[1],
        "offs": striped(idx),
        "offs2": striped(idx2),
        "offs3": striped(idx3),
        "offs4": striped(idx4),
        "offs5": striped(idx5),
        "offs6": striped(idx6),
        "offs7": striped(idx7),
    }


def reference(xt_words, xt_scales, xo_words, xo_scales, w_words, w_scales, w2_words, w2_scales, sa, sb, sg, wb_words, wb_scales, ws_words, ws_scales, offs, offs2, offs3, offs4, offs5, offs6, offs7):
    idx = unstriped(offs)
    idx2 = unstriped(offs2)
    idx3 = unstriped(offs3)
    idx4 = unstriped(offs4)
    idx5 = unstriped(offs5)
    idx6 = unstriped(offs6)
    idx7 = unstriped(offs7)
    xtu = unpack_weight(xt_words, xt_scales, "e2m1")
    xou = unpack_weight(xo_words, xo_scales, "e4m3")
    wu = unpack_weight(w_words, w_scales, "e4m3")
    w2u = unpack_weight(w2_words, w2_scales, "e2m1")
    wbu = unpack_weight(wb_words, wb_scales, "e2m1")
    wsu = unpack_weight(ws_words, ws_scales, "e4m3")
    xtidxg = xtu[:, idx]
    a = wu.T @ xtidxg
    xoidx2g = xou[:, idx2]
    b = w2u.T @ xoidx2g
    lb = b[:, 0:1]
    hid = a[:, idx3] * f64(sa) * sigmoid(a[:, idx4] * f64(sg) + lb) - b[:, idx5] * f64(sb)
    hidq = mxq(hid, 0, "e5m2")
    xtidx6g = xtu[:, idx6]
    p = wbu.T @ hidq + wsu.T @ xtidx6g
    y = np.zeros((N, E))
    y[:, idx7] = p
    return y

@@ -1,0 +1,198 @@
+from contextlib import ExitStack
+
+import concourse.mybir as mybir
+
+K, T, J, R, F, Z, O, N, E = 512, 1024, 256, 512, 512, 1024, 128, 256, 1024
+FLOPS = 2 * K * R * J + 2 * F * R * J + 2 * R * N * O + 2 * K * N * O
+
+F32 = mybir.dt.float32
+BF16 = mybir.dt.bfloat16
+I32 = mybir.dt.int32
+U32 = mybir.dt.uint32
+U16 = mybir.dt.uint16
+U8 = mybir.dt.uint8
+E4M3X4 = mybir.dt.float8_e4m3fn_x4
+E5M2X4 = mybir.dt.float8_e5m2_x4
+E2M1X4 = mybir.dt.float4_e2m1fn_x4
+ACT = mybir.ActivationFunctionType
+ALU = mybir.AluOpType
+
+P = 128
+PACK = 4
+QUAD = 32
+
+
+def tile_list_offsetlead_twotab_further_scattered_kernel(
+    tc, xt_words, xt_scales, xo_words, xo_scales, w_words, w_scales, w2_words, w2_scales, sa, sb, sg,
+    wb_words, wb_scales, ws_words, ws_scales, offs, offs2, offs3, offs4, offs5, offs6, offs7, out,
+):
+    nc = tc.nc
+    with ExitStack() as ctx:
+        lists = ctx.enter_context(tc.tile_pool(name="lists", bufs=1))
+        keep = ctx.enter_context(tc.tile_pool(name="keep", bufs=1))
+        psum = ctx.enter_context(tc.psum_pool(name="psum", bufs=1))
+
+        def sb_tile(shape, dtype, name):
+            return keep.tile(shape, dtype, name=name, align_bytes=64)
+
+        def load_list(src, name):
+            t = lists.tile([P, src.shape[1]], U16, name=name)
+            nc.sync.dma_start(t[:], src)
+            return t
+
+        def load_words(src, dtype, cols, name):
+            t = sb_tile([P, cols], dtype, name)
+            flat = src[0] if len(src.shape) == 3 else src[0].rearrange("p c r -> p (c r)")
+            nc.sync.dma_start(t[:].bitcast(I32), flat.bitcast(I32))
+            return t
+
+        def load_scale_rows(plane, src, q):
+            nc.sync.dma_start(plane[QUAD * q : QUAD * q + 4, :].bitcast(I32), src[0, 4 * q : 4 * q + 4, :].bitcast(I32))
+
+        def load_scale_pair(stage, src, c0, h):
+            cols = src.shape[2]
+            rows = src[0].rearrange("(j h r) c -> h r j c", j=2, h=2)[h]
+            nc.sync.dma_start(stage[QUAD * h : QUAD * h + 4, :, c0 : c0 + cols].bitcast(I32), rows.bitcast(I32))
+
+        def lift_upper_half(stage):
+            nc.vector.tensor_copy(stage[64:128, 0, :].bitcast(I32), stage[0:64, 1, :].bitcast(I32))
+
+        def load_rows(src, name):
+            t = sb_tile([P, PACK], F32, name)
+            nc.gpsimd.dma_start(t[:], src.rearrange("(p t) one -> p (t one)", t=PACK))
+            return t
+
+        ww_stage = sb_tile([P, 2, 2 * R], U8, "ww_stage")
+        xt_plane = sb_tile([P, T], U8, "xt_plane")
+        xo_plane = sb_tile([P, Z], U8, "xo_plane")
+        out_stage = sb_tile([P, 2, 2 * N], U8, "out_stage")
+        pages = [sb_tile([P, E], F32, "page%d" % h) for h in range(N // P)]
+        nc.vector.memset(ww_stage[0:64].rearrange("p j c -> p (j c)").bitcast(I32), 0)
+        nc.vector.memset(xt_plane[:].bitcast(I32), 0)
+        nc.vector.memset(xo_plane[:].bitcast(I32), 0)
+        nc.vector.memset(out_stage[0:64].rearrange("p j c -> p (j c)").bitcast(I32), 0)
+        for page in pages:
+            nc.vector.memset(page[:], 0.0)
+
+        sa_t = load_rows(sa, "sa_t")
+        sg_t = load_rows(sg, "sg_t")
+        sb_t = load_rows(sb, "sb_t")
+
+        l1 = load_list(offs, "l1")
+        for h in range(2):
+            load_scale_pair(ww_stage, w_scales, 0, h)
+        for h in range(2):
+            load_scale_pair(ww_stage, w2_scales, R, h)
+        load_scale_rows(xt_plane, xt_scales, 0)
+        xt_w = load_words(xt_words, U16, T, "xt_w")
+        w_w = load_words(w_words, U32, R, "w_w")
+        for q in range(1, 4):
+            load_scale_rows(xt_plane, xt_scales, q)
+        w2_w = load_words(w2_words, U16, R, "w2_w")
+        xo_w = load_words(xo_words, U32, Z, "xo_w")
+        l2 = load_list(offs2, "l2")
+        for q in range(4):
+            load_scale_rows(xo_plane, xo_scales, q)
+        l3 = load_list(offs3, "l3")
+        l4 = load_list(offs4, "l4")
+        l5 = load_list(offs5, "l5")
+        l6 = load_list(offs6, "l6")
+        ws_w = load_words(ws_words, U32, N, "ws_w")
+        wb_w = load_words(wb_words, U16, N, "wb_w")
+        for h in range(2):
+            load_scale_pair(out_stage, ws_scales, 0, h)
+        for h in range(2):
+            load_scale_pair(out_stage, wb_scales, N, h)
+        l7 = load_list(offs7, "l7")
+
+        lift_upper_half(ww_stage)
+        ww_plane = sb_tile([P, 2, PACK, P], U8, "ww_plane")
+        nc.vector.tensor_copy(
+            ww_plane[:].rearrange("p a t m -> p a m t"),
+            ww_stage[:, 0, :].rearrange("p (a m t) -> p a m t", a=2, t=PACK),
+        )
+        w_dealt = sb_tile([P, PACK, P], U32, "w_dealt")
+        nc.scalar.copy(w_dealt[:].rearrange("p t m -> p m t"), w_w[:].rearrange("p (m t) -> p m t", t=PACK))
+        w2_dealt = sb_tile([P, PACK, P], U16, "w2_dealt")
+        nc.scalar.copy(w2_dealt[:].rearrange("p t m -> p m t"), w2_w[:].rearrange("p (m t) -> p m t", t=PACK))
+
+        def pick(words, plane, lst, dtype, count, name):
+            picked_w = sb_tile([P, count], dtype, name + "_w")
+            picked_s = sb_tile([P, count], U8, name + "_s")
+            nc.vector.tensor_copy(picked_w[:], words[:].indirect(lst[:]))
+            nc.vector.tensor_copy(picked_s[:], plane[:].indirect(lst[:]))
+            return picked_w, picked_s
+
+        x1_w, x1_s = pick(xt_w, xt_plane, l1, U16, J, "x1")
+        a_ps = [psum.tile([P, J], F32, name="a_ps%d" % t, tag="bank%d" % t) for t in range(PACK)]
+        for t in range(PACK):
+            nc.tensor.matmul_mx(
+                a_ps[t][:], lhsT=w_dealt[:, t, :].bitcast(E4M3X4), lhsT_scale=ww_plane[:, 0, t, :],
+                rhs=x1_w[:].bitcast(E2M1X4), rhs_scale=x1_s[:], start=True, stop=True,
+            )
+        x2_w, x2_s = pick(xo_w, xo_plane, l2, U32, J, "x2")
+        b_ps = [psum.tile([P, J], F32, name="b_ps%d" % t, tag="bank%d" % (PACK + t)) for t in range(PACK)]
+        for t in range(PACK):
+            nc.tensor.matmul_mx(
+                b_ps[t][:], lhsT=w2_dealt[:, t, :].bitcast(E2M1X4), lhsT_scale=ww_plane[:, 1, t, :],
+                rhs=x2_w[:].bitcast(E4M3X4), rhs_scale=x2_s[:], start=True, stop=True,
+            )
+
+        a_sb = [sb_tile([P, J], F32, "a_sb%d" % t) for t in range(PACK)]
+        b_sb = [sb_tile([P, J], F32, "b_sb%d" % t) for t in range(PACK)]
+        lin = sb_tile([P, PACK, O], F32, "lin")
+        gate = sb_tile([P, PACK, O], F32, "gate")
+        sub = sb_tile([P, PACK, O], F32, "sub")
+        gated = sb_tile([P, PACK, O], F32, "gated")
+        hid = sb_tile([P, O, PACK], BF16, "hid")
+
+        nc.scalar.copy(a_sb[0][:], a_ps[0][:])
+        for t in range(PACK):
+            if t + 1 < PACK:
+                nc.scalar.copy(a_sb[t + 1][:], a_ps[t + 1][:])
+            nc.scalar.activation(lin[:, t, :], a_sb[t][:].indirect(l3[:]), ACT.Copy, scale=sa_t[:, t : t + 1])
+        for t in range(PACK):
+            nc.vector.tensor_copy(b_sb[t][:], b_ps[t][:])
+        for t in range(PACK):
+            nc.scalar.activation(
+                gate[:, t, :], a_sb[t][:].indirect(l4[:]), ACT.Sigmoid, bias=b_sb[t][:, 0:1], scale=sg_t[:, t : t + 1]
+            )
+        for t in range(PACK):
+            nc.scalar.activation(sub[:, t, :], b_sb[t][:].indirect(l5[:]), ACT.Copy, scale=sb_t[:, t : t + 1])
+
+        x6_w, x6_s = pick(xt_w, xt_plane, l6, U16, O, "x6")
+        lift_upper_half(out_stage)
+        p_ps = [psum.tile([P, O], F32, name="p_ps%d" % h, tag="bank%d" % h) for h in range(N // P)]
+        for h in range(N // P):
+            cols = slice(h * P, (h + 1) * P)
+            nc.tensor.matmul_mx(
+                p_ps[h][:], lhsT=ws_w[:, cols].bitcast(E4M3X4), lhsT_scale=out_stage[:, 0, cols],
+                rhs=x6_w[:].bitcast(E2M1X4), rhs_scale=x6_s[:], start=True, stop=False,
+            )
+
+        for u in range(2):
+            pair = slice(2 * u, 2 * u + 2)
+            nc.vector.tensor_tensor(gated[:, pair, :], lin[:, pair, :], gate[:, pair, :], ALU.mult)
+        for u in range(2):
+            pair = slice(2 * u, 2 * u + 2)
+            nc.vector.tensor_tensor(
+                hid[:, :, pair], gated[:, pair, :].rearrange("p t o -> p o t"),
+                sub[:, pair, :].rearrange("p t o -> p o t"), ALU.subtract,
+            )
+        hid_w = sb_tile([P, O], U32, "hid_w")
+        hid_s = sb_tile([P, O], U8, "hid_s")
+        nc.vector.quantize_mx(out=hid_w[:].bitcast(E5M2X4), scales=hid_s[:], in_=hid[:].rearrange("p o t -> p (o t)"))
+        for h in range(N // P):
+            cols = slice(h * P, (h + 1) * P)
+            nc.tensor.matmul_mx(
+                p_ps[h][:], lhsT=wb_w[:, cols].bitcast(E2M1X4), lhsT_scale=out_stage[:, 0, N + h * P : N + (h + 1) * P],
+                rhs=hid_w[:].bitcast(E5M2X4), rhs_scale=hid_s[:], start=False, stop=True,
+            )
+
+        p_sb = [sb_tile([P, O], F32, "p_sb%d" % h) for h in range(N // P)]
+        nc.vector.tensor_copy(p_sb[0][:], p_ps[0][:])
+        nc.scalar.copy(p_sb[1][:], p_ps[1][:])
+        nc.vector.tensor_copy(pages[0][:].indirect(l7[:]), p_sb[0][:])
+        nc.scalar.activation(pages[1][:].indirect(l7[:]), p_sb[1][:], ACT.Copy)
+        nc.sync.dma_start(out[0:P, :], pages[0][:])
+        nc.scalar.dma_start(out[P : 2 * P, :], pages[1][:])

@@ -62,15 +62,21 @@ def tile_list_offsetlead_twotab_further_scattered_kernel(
             nc.gpsimd.dma_start(t[:], src.rearrange("(p t) one -> p (t one)", t=PACK))
             return t
 
-        ww_stage = sb_tile([P, 2, 2 * R], U8, "ww_stage")
+        ww_rows = sb_tile([4, 4, 2 * R], U8, "ww_rows")
+        ww_spread = sb_tile([P, 2 * R], U8, "ww_spread")
         xt_plane = sb_tile([P, T], U8, "xt_plane")
         xo_plane = sb_tile([P, Z], U8, "xo_plane")
         out_stage = sb_tile([P, 2, 2 * N], U8, "out_stage")
         pages = [sb_tile([P, E], F32, "page%d" % h) for h in range(N // P)]
-        nc.vector.memset(ww_stage[0:64].rearrange("p j c -> p (j c)").bitcast(I32), 0)
-        nc.vector.memset(xt_plane[:].bitcast(I32), 0)
+
+        warm_in = sb_tile([P, 1], F32, "warm_in")
+        warm_out = sb_tile([P, 1], F32, "warm_out")
+        nc.vector.memset(warm_in[:], 0.0)
+        nc.scalar.activation(warm_out[:], warm_in[:], ACT.Sigmoid)
+
         nc.vector.memset(xo_plane[:].bitcast(I32), 0)
         nc.vector.memset(out_stage[0:64].rearrange("p j c -> p (j c)").bitcast(I32), 0)
+        nc.vector.memset(ww_spread[:].bitcast(I32), 0)
         for page in pages:
             nc.vector.memset(page[:], 0.0)
 
@@ -79,18 +85,18 @@ def tile_list_offsetlead_twotab_further_scattered_kernel(
         sb_t = load_rows(sb, "sb_t")
 
         l1 = load_list(offs, "l1")
-        for h in range(2):
-            load_scale_pair(ww_stage, w_scales, 0, h)
-        for h in range(2):
-            load_scale_pair(ww_stage, w2_scales, R, h)
-        load_scale_rows(xt_plane, xt_scales, 0)
+        for i, src in enumerate((w_scales, w2_scales)):
+            nc.sync.dma_start(
+                ww_rows[:, :, i * R : (i + 1) * R].bitcast(I32), src[0].rearrange("(q r) c -> r q c", r=4).bitcast(I32)
+            )
+        for q in range(4):
+            rows = xt_scales[0, 4 * q : 4 * q + 4, :].bitcast(I32)
+            nc.sync.dma_start(xt_plane[QUAD * q : QUAD * (q + 1), :].bitcast(I32), rows.unsqueeze(0).to_broadcast([8, 4, T // 4]))
         xt_w = load_words(xt_words, U16, T, "xt_w")
         w_w = load_words(w_words, U32, R, "w_w")
-        for q in range(1, 4):
-            load_scale_rows(xt_plane, xt_scales, q)
+        l2 = load_list(offs2, "l2")
         w2_w = load_words(w2_words, U16, R, "w2_w")
         xo_w = load_words(xo_words, U32, Z, "xo_w")
-        l2 = load_list(offs2, "l2")
         for q in range(4):
             load_scale_rows(xo_plane, xo_scales, q)
         l3 = load_list(offs3, "l3")
@@ -105,11 +111,12 @@ def tile_list_offsetlead_twotab_further_scattered_kernel(
             load_scale_pair(out_stage, wb_scales, N, h)
         l7 = load_list(offs7, "l7")
 
-        lift_upper_half(ww_stage)
+        for q in range(4):
+            nc.vector.tensor_copy(ww_spread[QUAD * q : QUAD * q + 4, :].bitcast(I32), ww_rows[:, q, :].bitcast(I32))
         ww_plane = sb_tile([P, 2, PACK, P], U8, "ww_plane")
         nc.vector.tensor_copy(
             ww_plane[:].rearrange("p a t m -> p a m t"),
-            ww_stage[:, 0, :].rearrange("p (a m t) -> p a m t", a=2, t=PACK),
+            ww_spread[:].rearrange("p (a m t) -> p a m t", a=2, t=PACK),
         )
         w_dealt = sb_tile([P, PACK, P], U32, "w_dealt")
         nc.scalar.copy(w_dealt[:].rearrange("p t m -> p m t"), w_w[:].rearrange("p (m t) -> p m t", t=PACK))
@@ -146,10 +153,12 @@ def tile_list_offsetlead_twotab_further_scattered_kernel(
         gated = sb_tile([P, PACK, O], F32, "gated")
         hid = sb_tile([P, O, PACK], BF16, "hid")
 
-        nc.scalar.copy(a_sb[0][:], a_ps[0][:])
         for t in range(PACK):
-            if t + 1 < PACK:
-                nc.scalar.copy(a_sb[t + 1][:], a_ps[t + 1][:])
+            if t < 2:
+                nc.scalar.copy(a_sb[t][:], a_ps[t][:])
+            else:
+                nc.vector.tensor_copy(a_sb[t][:], a_ps[t][:])
+        for t in range(PACK):
             nc.scalar.activation(lin[:, t, :], a_sb[t][:].indirect(l3[:]), ACT.Copy, scale=sa_t[:, t : t + 1])
         for t in range(PACK):
             nc.vector.tensor_copy(b_sb[t][:], b_ps[t][:])

@@ -32,8 +32,8 @@ def tile_list_offsetlead_twotab_further_scattered_kernel(
         keep = ctx.enter_context(tc.tile_pool(name="keep", bufs=1))
         psum = ctx.enter_context(tc.psum_pool(name="psum", bufs=1))
 
-        def sb_tile(shape, dtype, name):
-            return keep.tile(shape, dtype, name=name, align_bytes=64)
+        def sb_tile(shape, dtype, name, tag=None):
+            return keep.tile(shape, dtype, name=name, tag=tag or name, align_bytes=64)
 
         def load_list(src, name):
             t = lists.tile([P, src.shape[1]], U16, name=name)
@@ -62,41 +62,40 @@ def tile_list_offsetlead_twotab_further_scattered_kernel(
             nc.gpsimd.dma_start(t[:], src.rearrange("(p t) one -> p (t one)", t=PACK))
             return t
 
-        ww_rows = sb_tile([4, 4, 2 * R], U8, "ww_rows")
-        ww_spread = sb_tile([P, 2 * R], U8, "ww_spread")
+        ww_stage = sb_tile([P, 2, 2 * R], U8, "ww_stage")
         xt_plane = sb_tile([P, T], U8, "xt_plane")
         xo_plane = sb_tile([P, Z], U8, "xo_plane")
-        out_stage = sb_tile([P, 2, 2 * N], U8, "out_stage")
+        ws_plane = sb_tile([P, N], U8, "ws_plane")
+        wb_plane = sb_tile([P, N], U8, "wb_plane")
         pages = [sb_tile([P, E], F32, "page%d" % h) for h in range(N // P)]
+        nc.vector.memset(ww_stage[0:64].rearrange("p j c -> p (j c)").bitcast(I32), 0)
+        for plane in (xt_plane, xo_plane, ws_plane, wb_plane):
+            nc.vector.memset(plane[:].bitcast(I32), 0)
+        for page in pages:
+            nc.vector.memset(page[:], 0.0)
 
         warm_in = sb_tile([P, 1], F32, "warm_in")
         warm_out = sb_tile([P, 1], F32, "warm_out")
-        nc.vector.memset(warm_in[:], 0.0)
+        nc.gpsimd.memset(warm_in[:], 0.0)
         nc.scalar.activation(warm_out[:], warm_in[:], ACT.Sigmoid)
-
-        nc.vector.memset(xo_plane[:].bitcast(I32), 0)
-        nc.vector.memset(out_stage[0:64].rearrange("p j c -> p (j c)").bitcast(I32), 0)
-        nc.vector.memset(ww_spread[:].bitcast(I32), 0)
-        for page in pages:
-            nc.vector.memset(page[:], 0.0)
 
         sa_t = load_rows(sa, "sa_t")
         sg_t = load_rows(sg, "sg_t")
         sb_t = load_rows(sb, "sb_t")
 
         l1 = load_list(offs, "l1")
-        for i, src in enumerate((w_scales, w2_scales)):
-            nc.sync.dma_start(
-                ww_rows[:, :, i * R : (i + 1) * R].bitcast(I32), src[0].rearrange("(q r) c -> r q c", r=4).bitcast(I32)
-            )
-        for q in range(4):
-            rows = xt_scales[0, 4 * q : 4 * q + 4, :].bitcast(I32)
-            nc.sync.dma_start(xt_plane[QUAD * q : QUAD * (q + 1), :].bitcast(I32), rows.unsqueeze(0).to_broadcast([8, 4, T // 4]))
+        for h in range(2):
+            load_scale_pair(ww_stage, w_scales, 0, h)
+        for h in range(2):
+            load_scale_pair(ww_stage, w2_scales, R, h)
+        load_scale_rows(xt_plane, xt_scales, 0)
         xt_w = load_words(xt_words, U16, T, "xt_w")
         w_w = load_words(w_words, U32, R, "w_w")
-        l2 = load_list(offs2, "l2")
+        for q in range(1, 4):
+            load_scale_rows(xt_plane, xt_scales, q)
         w2_w = load_words(w2_words, U16, R, "w2_w")
         xo_w = load_words(xo_words, U32, Z, "xo_w")
+        l2 = load_list(offs2, "l2")
         for q in range(4):
             load_scale_rows(xo_plane, xo_scales, q)
         l3 = load_list(offs3, "l3")
@@ -105,47 +104,48 @@ def tile_list_offsetlead_twotab_further_scattered_kernel(
         l6 = load_list(offs6, "l6")
         ws_w = load_words(ws_words, U32, N, "ws_w")
         wb_w = load_words(wb_words, U16, N, "wb_w")
-        for h in range(2):
-            load_scale_pair(out_stage, ws_scales, 0, h)
-        for h in range(2):
-            load_scale_pair(out_stage, wb_scales, N, h)
         l7 = load_list(offs7, "l7")
-
         for q in range(4):
-            nc.vector.tensor_copy(ww_spread[QUAD * q : QUAD * q + 4, :].bitcast(I32), ww_rows[:, q, :].bitcast(I32))
-        ww_plane = sb_tile([P, 2, PACK, P], U8, "ww_plane")
-        nc.vector.tensor_copy(
-            ww_plane[:].rearrange("p a t m -> p a m t"),
-            ww_spread[:].rearrange("p (a m t) -> p a m t", a=2, t=PACK),
-        )
+            load_scale_rows(ws_plane, ws_scales, q)
+        for q in range(4):
+            load_scale_rows(wb_plane, wb_scales, q)
+
         w_dealt = sb_tile([P, PACK, P], U32, "w_dealt")
         nc.scalar.copy(w_dealt[:].rearrange("p t m -> p m t"), w_w[:].rearrange("p (m t) -> p m t", t=PACK))
         w2_dealt = sb_tile([P, PACK, P], U16, "w2_dealt")
         nc.scalar.copy(w2_dealt[:].rearrange("p t m -> p m t"), w2_w[:].rearrange("p (m t) -> p m t", t=PACK))
 
-        def pick(words, plane, lst, dtype, count, name):
-            picked_w = sb_tile([P, count], dtype, name + "_w")
-            picked_s = sb_tile([P, count], U8, name + "_s")
-            nc.vector.tensor_copy(picked_w[:], words[:].indirect(lst[:]))
-            nc.vector.tensor_copy(picked_s[:], plane[:].indirect(lst[:]))
-            return picked_w, picked_s
+        def pick(window, lst, dtype, count, name, tag=None):
+            picked = sb_tile([P, count], dtype, name, tag)
+            nc.vector.tensor_copy(picked[:], window[:].indirect(lst[:]))
+            return picked
 
-        x1_w, x1_s = pick(xt_w, xt_plane, l1, U16, J, "x1")
+        def deal_plane(c0, name):
+            plane = sb_tile([P, PACK, P], U8, name)
+            nc.vector.tensor_copy(plane[:], ww_stage[:, 0, c0 : c0 + R].rearrange("p (m t) -> p t m", t=PACK))
+            return plane
+
+        lift_upper_half(ww_stage)
+        w_plane = deal_plane(0, "w_plane")
+        x1_w = pick(xt_w, l1, U16, J, "x1_w")
+        x1_s = pick(xt_plane, l1, U8, J, "x1_s")
+        w2_plane = deal_plane(R, "w2_plane")
+        x2_w = pick(xo_w, l2, U32, J, "x2_w")
+        x2_s = pick(xo_plane, l2, U8, J, "x2_s")
         a_ps = [psum.tile([P, J], F32, name="a_ps%d" % t, tag="bank%d" % t) for t in range(PACK)]
         for t in range(PACK):
             nc.tensor.matmul_mx(
-                a_ps[t][:], lhsT=w_dealt[:, t, :].bitcast(E4M3X4), lhsT_scale=ww_plane[:, 0, t, :],
+                a_ps[t][:], lhsT=w_dealt[:, t, :].bitcast(E4M3X4), lhsT_scale=w_plane[:, t, :],
                 rhs=x1_w[:].bitcast(E2M1X4), rhs_scale=x1_s[:], start=True, stop=True,
             )
-        x2_w, x2_s = pick(xo_w, xo_plane, l2, U32, J, "x2")
         b_ps = [psum.tile([P, J], F32, name="b_ps%d" % t, tag="bank%d" % (PACK + t)) for t in range(PACK)]
         for t in range(PACK):
             nc.tensor.matmul_mx(
-                b_ps[t][:], lhsT=w2_dealt[:, t, :].bitcast(E2M1X4), lhsT_scale=ww_plane[:, 1, t, :],
+                b_ps[t][:], lhsT=w2_dealt[:, t, :].bitcast(E2M1X4), lhsT_scale=w2_plane[:, t, :],
                 rhs=x2_w[:].bitcast(E4M3X4), rhs_scale=x2_s[:], start=True, stop=True,
             )
 
-        a_sb = [sb_tile([P, J], F32, "a_sb%d" % t) for t in range(PACK)]
+        a_sb = [sb_tile([P, J], F32, "a_sb%d" % t, {2: "xo_plane", 3: "xo_w"}.get(t)) for t in range(PACK)]
         b_sb = [sb_tile([P, J], F32, "b_sb%d" % t) for t in range(PACK)]
         lin = sb_tile([P, PACK, O], F32, "lin")
         gate = sb_tile([P, PACK, O], F32, "gate")
@@ -169,13 +169,13 @@ def tile_list_offsetlead_twotab_further_scattered_kernel(
         for t in range(PACK):
             nc.scalar.activation(sub[:, t, :], b_sb[t][:].indirect(l5[:]), ACT.Copy, scale=sb_t[:, t : t + 1])
 
-        x6_w, x6_s = pick(xt_w, xt_plane, l6, U16, O, "x6")
-        lift_upper_half(out_stage)
+        x6_w = pick(xt_w, l6, U16, O, "x6_w", "x2_w")
+        x6_s = pick(xt_plane, l6, U8, O, "x6_s", "x2_s")
         p_ps = [psum.tile([P, O], F32, name="p_ps%d" % h, tag="bank%d" % h) for h in range(N // P)]
         for h in range(N // P):
             cols = slice(h * P, (h + 1) * P)
             nc.tensor.matmul_mx(
-                p_ps[h][:], lhsT=ws_w[:, cols].bitcast(E4M3X4), lhsT_scale=out_stage[:, 0, cols],
+                p_ps[h][:], lhsT=ws_w[:, cols].bitcast(E4M3X4), lhsT_scale=ws_plane[:, cols],
                 rhs=x6_w[:].bitcast(E2M1X4), rhs_scale=x6_s[:], start=True, stop=False,
             )
 
@@ -194,7 +194,7 @@ def tile_list_offsetlead_twotab_further_scattered_kernel(
         for h in range(N // P):
             cols = slice(h * P, (h + 1) * P)
             nc.tensor.matmul_mx(
-                p_ps[h][:], lhsT=wb_w[:, cols].bitcast(E2M1X4), lhsT_scale=out_stage[:, 0, N + h * P : N + (h + 1) * P],
+                p_ps[h][:], lhsT=wb_w[:, cols].bitcast(E2M1X4), lhsT_scale=wb_plane[:, cols],
                 rhs=hid_w[:].bitcast(E5M2X4), rhs_scale=hid_s[:], start=False, stop=True,
             )
 

@@ -18,8 +18,13 @@ ACT = mybir.ActivationFunctionType
 ALU = mybir.AluOpType
 
 P = 128
+HALF = P // 2
 PACK = 4
 QUAD = 32
+QUADS = P // QUAD
+ROWS = 4
+ROW_TILES = N // P
+A_ON_SCALAR = 3
 
 
 def tile_list_offsetlead_twotab_further_scattered_kernel(
@@ -36,39 +41,36 @@ def tile_list_offsetlead_twotab_further_scattered_kernel(
             return keep.tile(shape, dtype, name=name, tag=tag or name, align_bytes=64)
 
         def load_list(src, name):
-            t = lists.tile([P, src.shape[1]], U16, name=name)
-            nc.sync.dma_start(t[:], src)
-            return t
+            tile = lists.tile([P, src.shape[1]], U16, name=name)
+            nc.sync.dma_start(tile[:], src)
+            return tile
 
         def load_words(src, dtype, cols, name):
-            t = sb_tile([P, cols], dtype, name)
+            tile = sb_tile([P, cols], dtype, name)
             flat = src[0] if len(src.shape) == 3 else src[0].rearrange("p c r -> p (c r)")
-            nc.sync.dma_start(t[:].bitcast(I32), flat.bitcast(I32))
-            return t
+            nc.sync.dma_start(tile[:].bitcast(I32), flat.bitcast(I32))
+            return tile
 
         def load_scale_rows(plane, src, q):
-            nc.sync.dma_start(plane[QUAD * q : QUAD * q + 4, :].bitcast(I32), src[0, 4 * q : 4 * q + 4, :].bitcast(I32))
+            rows = src[0, ROWS * q : ROWS * (q + 1), :]
+            nc.sync.dma_start(plane[QUAD * q : QUAD * q + ROWS, :].bitcast(I32), rows.bitcast(I32))
 
-        def load_scale_pair(stage, src, c0, h):
-            cols = src.shape[2]
-            rows = src[0].rearrange("(j h r) c -> h r j c", j=2, h=2)[h]
-            nc.sync.dma_start(stage[QUAD * h : QUAD * h + 4, :, c0 : c0 + cols].bitcast(I32), rows.bitcast(I32))
-
-        def lift_upper_half(stage):
-            nc.vector.tensor_copy(stage[64:128, 0, :].bitcast(I32), stage[0:64, 1, :].bitcast(I32))
+        def load_scale_pair(stage, src, c0, q):
+            rows = src[0].rearrange("(j q r) c -> q r j c", j=2, q=2)[q]
+            nc.sync.dma_start(stage[QUAD * q : QUAD * q + ROWS, :, c0 : c0 + R].bitcast(I32), rows.bitcast(I32))
 
         def load_rows(src, name):
-            t = sb_tile([P, PACK], F32, name)
-            nc.gpsimd.dma_start(t[:], src.rearrange("(p t) one -> p (t one)", t=PACK))
-            return t
+            tile = sb_tile([P, PACK], F32, name)
+            nc.gpsimd.dma_start(tile[:], src.rearrange("(p t) one -> p (t one)", t=PACK))
+            return tile
 
         ww_stage = sb_tile([P, 2, 2 * R], U8, "ww_stage")
         xt_plane = sb_tile([P, T], U8, "xt_plane")
         xo_plane = sb_tile([P, Z], U8, "xo_plane")
         ws_plane = sb_tile([P, N], U8, "ws_plane")
         wb_plane = sb_tile([P, N], U8, "wb_plane")
-        pages = [sb_tile([P, E], F32, "page%d" % h) for h in range(N // P)]
-        nc.vector.memset(ww_stage[0:64].rearrange("p j c -> p (j c)").bitcast(I32), 0)
+        pages = [sb_tile([P, E], F32, "page%d" % h) for h in range(ROW_TILES)]
+        nc.vector.memset(ww_stage[0:HALF].rearrange("p j c -> p (j c)").bitcast(I32), 0)
         for plane in (xt_plane, xo_plane, ws_plane, wb_plane):
             nc.vector.memset(plane[:].bitcast(I32), 0)
         for page in pages:
@@ -83,31 +85,31 @@ def tile_list_offsetlead_twotab_further_scattered_kernel(
         sg_t = load_rows(sg, "sg_t")
         sb_t = load_rows(sb, "sb_t")
 
-        l1 = load_list(offs, "l1")
-        for h in range(2):
-            load_scale_pair(ww_stage, w_scales, 0, h)
-        for h in range(2):
-            load_scale_pair(ww_stage, w2_scales, R, h)
+        list1 = load_list(offs, "list1")
+        for q in range(2):
+            load_scale_pair(ww_stage, w_scales, 0, q)
+        for q in range(2):
+            load_scale_pair(ww_stage, w2_scales, R, q)
         load_scale_rows(xt_plane, xt_scales, 0)
         xt_w = load_words(xt_words, U16, T, "xt_w")
         w_w = load_words(w_words, U32, R, "w_w")
-        for q in range(1, 4):
+        for q in range(1, QUADS):
             load_scale_rows(xt_plane, xt_scales, q)
         w2_w = load_words(w2_words, U16, R, "w2_w")
         xo_w = load_words(xo_words, U32, Z, "xo_w")
-        l2 = load_list(offs2, "l2")
-        for q in range(4):
+        list2 = load_list(offs2, "list2")
+        for q in range(QUADS):
             load_scale_rows(xo_plane, xo_scales, q)
-        l3 = load_list(offs3, "l3")
-        l4 = load_list(offs4, "l4")
-        l5 = load_list(offs5, "l5")
-        l6 = load_list(offs6, "l6")
+        list3 = load_list(offs3, "list3")
+        list4 = load_list(offs4, "list4")
+        list5 = load_list(offs5, "list5")
+        list6 = load_list(offs6, "list6")
         ws_w = load_words(ws_words, U32, N, "ws_w")
         wb_w = load_words(wb_words, U16, N, "wb_w")
-        l7 = load_list(offs7, "l7")
-        for q in range(4):
+        list7 = load_list(offs7, "list7")
+        for q in range(QUADS):
             load_scale_rows(ws_plane, ws_scales, q)
-        for q in range(4):
+        for q in range(QUADS):
             load_scale_rows(wb_plane, wb_scales, q)
 
         w_dealt = sb_tile([P, PACK, P], U32, "w_dealt")
@@ -115,9 +117,9 @@ def tile_list_offsetlead_twotab_further_scattered_kernel(
         w2_dealt = sb_tile([P, PACK, P], U16, "w2_dealt")
         nc.scalar.copy(w2_dealt[:].rearrange("p t m -> p m t"), w2_w[:].rearrange("p (m t) -> p m t", t=PACK))
 
-        def pick(window, lst, dtype, count, name, tag=None):
+        def pick(window, offsets, dtype, count, name, tag=None):
             picked = sb_tile([P, count], dtype, name, tag)
-            nc.vector.tensor_copy(picked[:], window[:].indirect(lst[:]))
+            nc.vector.tensor_copy(picked[:], window[:].indirect(offsets[:]))
             return picked
 
         def deal_plane(c0, name):
@@ -125,13 +127,14 @@ def tile_list_offsetlead_twotab_further_scattered_kernel(
             nc.vector.tensor_copy(plane[:], ww_stage[:, 0, c0 : c0 + R].rearrange("p (m t) -> p t m", t=PACK))
             return plane
 
-        lift_upper_half(ww_stage)
+        nc.vector.tensor_copy(ww_stage[HALF:P, 0, :].bitcast(I32), ww_stage[0:HALF, 1, :].bitcast(I32))
         w_plane = deal_plane(0, "w_plane")
-        x1_w = pick(xt_w, l1, U16, J, "x1_w")
-        x1_s = pick(xt_plane, l1, U8, J, "x1_s")
+        x1_w = pick(xt_w, list1, U16, J, "x1_w")
+        x1_s = pick(xt_plane, list1, U8, J, "x1_s")
         w2_plane = deal_plane(R, "w2_plane")
-        x2_w = pick(xo_w, l2, U32, J, "x2_w")
-        x2_s = pick(xo_plane, l2, U8, J, "x2_s")
+        x2_w = pick(xo_w, list2, U32, J, "x2_w")
+        x2_s = pick(xo_plane, list2, U8, J, "x2_s")
+
         a_ps = [psum.tile([P, J], F32, name="a_ps%d" % t, tag="bank%d" % t) for t in range(PACK)]
         for t in range(PACK):
             nc.tensor.matmul_mx(
@@ -145,63 +148,62 @@ def tile_list_offsetlead_twotab_further_scattered_kernel(
                 rhs=x2_w[:].bitcast(E4M3X4), rhs_scale=x2_s[:], start=True, stop=True,
             )
 
-        a_sb = [sb_tile([P, J], F32, "a_sb%d" % t, {2: "xo_plane", 3: "xo_w"}.get(t)) for t in range(PACK)]
+        a_sb = [sb_tile([P, J], F32, "a_sb%d" % t, None if t < A_ON_SCALAR else "xo_plane") for t in range(PACK)]
         b_sb = [sb_tile([P, J], F32, "b_sb%d" % t) for t in range(PACK)]
-        lin = sb_tile([P, PACK, O], F32, "lin")
+        a_scaled = sb_tile([P, PACK, O], F32, "a_scaled")
         gate = sb_tile([P, PACK, O], F32, "gate")
-        sub = sb_tile([P, PACK, O], F32, "sub")
+        b_scaled = sb_tile([P, PACK, O], F32, "b_scaled")
         gated = sb_tile([P, PACK, O], F32, "gated")
         hid = sb_tile([P, O, PACK], BF16, "hid")
 
+        for t in range(A_ON_SCALAR):
+            nc.scalar.copy(a_sb[t][:], a_ps[t][:])
+        for t in range(A_ON_SCALAR, PACK):
+            nc.vector.tensor_copy(a_sb[t][:], a_ps[t][:])
         for t in range(PACK):
-            if t < 2:
-                nc.scalar.copy(a_sb[t][:], a_ps[t][:])
-            else:
-                nc.vector.tensor_copy(a_sb[t][:], a_ps[t][:])
-        for t in range(PACK):
-            nc.scalar.activation(lin[:, t, :], a_sb[t][:].indirect(l3[:]), ACT.Copy, scale=sa_t[:, t : t + 1])
+            nc.scalar.activation(a_scaled[:, t, :], a_sb[t][:].indirect(list3[:]), ACT.Copy, scale=sa_t[:, t : t + 1])
         for t in range(PACK):
             nc.vector.tensor_copy(b_sb[t][:], b_ps[t][:])
         for t in range(PACK):
             nc.scalar.activation(
-                gate[:, t, :], a_sb[t][:].indirect(l4[:]), ACT.Sigmoid, bias=b_sb[t][:, 0:1], scale=sg_t[:, t : t + 1]
+                gate[:, t, :], a_sb[t][:].indirect(list4[:]), ACT.Sigmoid,
+                bias=b_sb[t][:, 0:1], scale=sg_t[:, t : t + 1],
             )
         for t in range(PACK):
-            nc.scalar.activation(sub[:, t, :], b_sb[t][:].indirect(l5[:]), ACT.Copy, scale=sb_t[:, t : t + 1])
+            nc.scalar.activation(b_scaled[:, t, :], b_sb[t][:].indirect(list5[:]), ACT.Copy, scale=sb_t[:, t : t + 1])
 
-        x6_w = pick(xt_w, l6, U16, O, "x6_w", "x2_w")
-        x6_s = pick(xt_plane, l6, U8, O, "x6_s", "x2_s")
-        p_ps = [psum.tile([P, O], F32, name="p_ps%d" % h, tag="bank%d" % h) for h in range(N // P)]
-        for h in range(N // P):
+        x6_w = pick(xt_w, list6, U16, O, "x6_w", "x2_w")
+        x6_s = pick(xt_plane, list6, U8, O, "x6_s", "x2_s")
+        p_ps = [psum.tile([P, O], F32, name="p_ps%d" % h, tag="bank%d" % h) for h in range(ROW_TILES)]
+        for h in range(ROW_TILES):
             cols = slice(h * P, (h + 1) * P)
             nc.tensor.matmul_mx(
                 p_ps[h][:], lhsT=ws_w[:, cols].bitcast(E4M3X4), lhsT_scale=ws_plane[:, cols],
                 rhs=x6_w[:].bitcast(E2M1X4), rhs_scale=x6_s[:], start=True, stop=False,
             )
 
-        for u in range(2):
-            pair = slice(2 * u, 2 * u + 2)
-            nc.vector.tensor_tensor(gated[:, pair, :], lin[:, pair, :], gate[:, pair, :], ALU.mult)
-        for u in range(2):
-            pair = slice(2 * u, 2 * u + 2)
+        pairs = [slice(t, t + 2) for t in range(0, PACK, 2)]
+        for pair in pairs:
+            nc.vector.tensor_tensor(gated[:, pair, :], a_scaled[:, pair, :], gate[:, pair, :], ALU.mult)
+        for pair in pairs:
             nc.vector.tensor_tensor(
                 hid[:, :, pair], gated[:, pair, :].rearrange("p t o -> p o t"),
-                sub[:, pair, :].rearrange("p t o -> p o t"), ALU.subtract,
+                b_scaled[:, pair, :].rearrange("p t o -> p o t"), ALU.subtract,
             )
         hid_w = sb_tile([P, O], U32, "hid_w")
         hid_s = sb_tile([P, O], U8, "hid_s")
         nc.vector.quantize_mx(out=hid_w[:].bitcast(E5M2X4), scales=hid_s[:], in_=hid[:].rearrange("p o t -> p (o t)"))
-        for h in range(N // P):
+        for h in range(ROW_TILES):
             cols = slice(h * P, (h + 1) * P)
             nc.tensor.matmul_mx(
                 p_ps[h][:], lhsT=wb_w[:, cols].bitcast(E2M1X4), lhsT_scale=wb_plane[:, cols],
                 rhs=hid_w[:].bitcast(E5M2X4), rhs_scale=hid_s[:], start=False, stop=True,
             )
 
-        p_sb = [sb_tile([P, O], F32, "p_sb%d" % h) for h in range(N // P)]
+        p_sb = [sb_tile([P, O], F32, "p_sb%d" % h) for h in range(ROW_TILES)]
         nc.vector.tensor_copy(p_sb[0][:], p_ps[0][:])
         nc.scalar.copy(p_sb[1][:], p_ps[1][:])
-        nc.vector.tensor_copy(pages[0][:].indirect(l7[:]), p_sb[0][:])
-        nc.scalar.activation(pages[1][:].indirect(l7[:]), p_sb[1][:], ACT.Copy)
+        nc.vector.tensor_copy(pages[0][:].indirect(list7[:]), p_sb[0][:])
+        nc.scalar.activation(pages[1][:].indirect(list7[:]), p_sb[1][:], ACT.Copy)
         nc.sync.dma_start(out[0:P, :], pages[0][:])
         nc.scalar.dma_start(out[P : 2 * P, :], pages[1][:])

from contextlib import ExitStack

import concourse.mybir as mybir

K, T, J, R, F, Z, O, N, E = 512, 1024, 256, 512, 512, 1024, 128, 256, 1024
FLOPS = 2 * K * R * J + 2 * F * R * J + 2 * R * N * O + 2 * K * N * O

F32 = mybir.dt.float32
BF16 = mybir.dt.bfloat16
I32 = mybir.dt.int32
U32 = mybir.dt.uint32
U16 = mybir.dt.uint16
U8 = mybir.dt.uint8
E4M3X4 = mybir.dt.float8_e4m3fn_x4
E5M2X4 = mybir.dt.float8_e5m2_x4
E2M1X4 = mybir.dt.float4_e2m1fn_x4
ACT = mybir.ActivationFunctionType
ALU = mybir.AluOpType

P = 128
HALF = P // 2
PACK = 4
QUAD = 32
QUADS = P // QUAD
ROWS = 4
ROW_TILES = N // P
A_ON_SCALAR = 3


def tile_list_offsetlead_twotab_further_scattered_kernel(
    tc, xt_words, xt_scales, xo_words, xo_scales, w_words, w_scales, w2_words, w2_scales, sa, sb, sg,
    wb_words, wb_scales, ws_words, ws_scales, offs, offs2, offs3, offs4, offs5, offs6, offs7, out,
):
    nc = tc.nc
    with ExitStack() as ctx:
        lists = ctx.enter_context(tc.tile_pool(name="lists", bufs=1))
        keep = ctx.enter_context(tc.tile_pool(name="keep", bufs=1))
        psum = ctx.enter_context(tc.psum_pool(name="psum", bufs=1))

        def sb_tile(shape, dtype, name, tag=None):
            return keep.tile(shape, dtype, name=name, tag=tag or name, align_bytes=64)

        def load_list(src, name):
            tile = lists.tile([P, src.shape[1]], U16, name=name)
            nc.sync.dma_start(tile[:], src)
            return tile

        def load_words(src, dtype, cols, name):
            tile = sb_tile([P, cols], dtype, name)
            flat = src[0] if len(src.shape) == 3 else src[0].rearrange("p c r -> p (c r)")
            nc.sync.dma_start(tile[:].bitcast(I32), flat.bitcast(I32))
            return tile

        def load_scale_rows(plane, src, q):
            rows = src[0, ROWS * q : ROWS * (q + 1), :]
            nc.sync.dma_start(plane[QUAD * q : QUAD * q + ROWS, :].bitcast(I32), rows.bitcast(I32))

        def load_scale_pair(stage, src, c0, q):
            rows = src[0].rearrange("(j q r) c -> q r j c", j=2, q=2)[q]
            nc.sync.dma_start(stage[QUAD * q : QUAD * q + ROWS, :, c0 : c0 + R].bitcast(I32), rows.bitcast(I32))

        def load_rows(src, name):
            tile = sb_tile([P, PACK], F32, name)
            nc.gpsimd.dma_start(tile[:], src.rearrange("(p t) one -> p (t one)", t=PACK))
            return tile

        ww_stage = sb_tile([P, 2, 2 * R], U8, "ww_stage")
        xt_plane = sb_tile([P, T], U8, "xt_plane")
        xo_plane = sb_tile([P, Z], U8, "xo_plane")
        ws_plane = sb_tile([P, N], U8, "ws_plane")
        wb_plane = sb_tile([P, N], U8, "wb_plane")
        pages = [sb_tile([P, E], F32, "page%d" % h) for h in range(ROW_TILES)]
        nc.vector.memset(ww_stage[0:HALF].rearrange("p j c -> p (j c)").bitcast(I32), 0)
        for plane in (xt_plane, xo_plane, ws_plane, wb_plane):
            nc.vector.memset(plane[:].bitcast(I32), 0)
        for page in pages:
            nc.vector.memset(page[:], 0.0)

        warm_in = sb_tile([P, 1], F32, "warm_in")
        warm_out = sb_tile([P, 1], F32, "warm_out")
        nc.gpsimd.memset(warm_in[:], 0.0)
        nc.scalar.activation(warm_out[:], warm_in[:], ACT.Sigmoid)

        sa_t = load_rows(sa, "sa_t")
        sg_t = load_rows(sg, "sg_t")
        sb_t = load_rows(sb, "sb_t")

        list1 = load_list(offs, "list1")
        for q in range(2):
            load_scale_pair(ww_stage, w_scales, 0, q)
        for q in range(2):
            load_scale_pair(ww_stage, w2_scales, R, q)
        load_scale_rows(xt_plane, xt_scales, 0)
        xt_w = load_words(xt_words, U16, T, "xt_w")
        w_w = load_words(w_words, U32, R, "w_w")
        for q in range(1, QUADS):
            load_scale_rows(xt_plane, xt_scales, q)
        w2_w = load_words(w2_words, U16, R, "w2_w")
        xo_w = load_words(xo_words, U32, Z, "xo_w")
        list2 = load_list(offs2, "list2")
        for q in range(QUADS):
            load_scale_rows(xo_plane, xo_scales, q)
        list3 = load_list(offs3, "list3")
        list4 = load_list(offs4, "list4")
        list5 = load_list(offs5, "list5")
        list6 = load_list(offs6, "list6")
        ws_w = load_words(ws_words, U32, N, "ws_w")
        wb_w = load_words(wb_words, U16, N, "wb_w")
        list7 = load_list(offs7, "list7")
        for q in range(QUADS):
            load_scale_rows(ws_plane, ws_scales, q)
        for q in range(QUADS):
            load_scale_rows(wb_plane, wb_scales, q)

        w_dealt = sb_tile([P, PACK, P], U32, "w_dealt")
        nc.scalar.copy(w_dealt[:].rearrange("p t m -> p m t"), w_w[:].rearrange("p (m t) -> p m t", t=PACK))
        w2_dealt = sb_tile([P, PACK, P], U16, "w2_dealt")
        nc.scalar.copy(w2_dealt[:].rearrange("p t m -> p m t"), w2_w[:].rearrange("p (m t) -> p m t", t=PACK))

        def pick(window, offsets, dtype, count, name, tag=None):
            picked = sb_tile([P, count], dtype, name, tag)
            nc.vector.tensor_copy(picked[:], window[:].indirect(offsets[:]))
            return picked

        def deal_plane(c0, name):
            plane = sb_tile([P, PACK, P], U8, name)
            nc.vector.tensor_copy(plane[:], ww_stage[:, 0, c0 : c0 + R].rearrange("p (m t) -> p t m", t=PACK))
            return plane

        nc.vector.tensor_copy(ww_stage[HALF:P, 0, :].bitcast(I32), ww_stage[0:HALF, 1, :].bitcast(I32))
        w_plane = deal_plane(0, "w_plane")
        x1_w = pick(xt_w, list1, U16, J, "x1_w")
        x1_s = pick(xt_plane, list1, U8, J, "x1_s")
        w2_plane = deal_plane(R, "w2_plane")
        x2_w = pick(xo_w, list2, U32, J, "x2_w")
        x2_s = pick(xo_plane, list2, U8, J, "x2_s")

        a_ps = [psum.tile([P, J], F32, name="a_ps%d" % t, tag="bank%d" % t) for t in range(PACK)]
        for t in range(PACK):
            nc.tensor.matmul_mx(
                a_ps[t][:], lhsT=w_dealt[:, t, :].bitcast(E4M3X4), lhsT_scale=w_plane[:, t, :],
                rhs=x1_w[:].bitcast(E2M1X4), rhs_scale=x1_s[:], start=True, stop=True,
            )
        b_ps = [psum.tile([P, J], F32, name="b_ps%d" % t, tag="bank%d" % (PACK + t)) for t in range(PACK)]
        for t in range(PACK):
            nc.tensor.matmul_mx(
                b_ps[t][:], lhsT=w2_dealt[:, t, :].bitcast(E2M1X4), lhsT_scale=w2_plane[:, t, :],
                rhs=x2_w[:].bitcast(E4M3X4), rhs_scale=x2_s[:], start=True, stop=True,
            )

        a_sb = [sb_tile([P, J], F32, "a_sb%d" % t, None if t < A_ON_SCALAR else "xo_plane") for t in range(PACK)]
        b_sb = [sb_tile([P, J], F32, "b_sb%d" % t) for t in range(PACK)]
        a_scaled = sb_tile([P, PACK, O], F32, "a_scaled")
        gate = sb_tile([P, PACK, O], F32, "gate")
        b_scaled = sb_tile([P, PACK, O], F32, "b_scaled")
        gated = sb_tile([P, PACK, O], F32, "gated")
        hid = sb_tile([P, O, PACK], BF16, "hid")

        for t in range(A_ON_SCALAR):
            nc.scalar.copy(a_sb[t][:], a_ps[t][:])
        for t in range(A_ON_SCALAR, PACK):
            nc.vector.tensor_copy(a_sb[t][:], a_ps[t][:])
        for t in range(PACK):
            nc.scalar.activation(a_scaled[:, t, :], a_sb[t][:].indirect(list3[:]), ACT.Copy, scale=sa_t[:, t : t + 1])
        for t in range(PACK):
            nc.vector.tensor_copy(b_sb[t][:], b_ps[t][:])
        for t in range(PACK):
            nc.scalar.activation(
                gate[:, t, :], a_sb[t][:].indirect(list4[:]), ACT.Sigmoid,
                bias=b_sb[t][:, 0:1], scale=sg_t[:, t : t + 1],
            )
        for t in range(PACK):
            nc.scalar.activation(b_scaled[:, t, :], b_sb[t][:].indirect(list5[:]), ACT.Copy, scale=sb_t[:, t : t + 1])

        x6_w = pick(xt_w, list6, U16, O, "x6_w", "x2_w")
        x6_s = pick(xt_plane, list6, U8, O, "x6_s", "x2_s")
        p_ps = [psum.tile([P, O], F32, name="p_ps%d" % h, tag="bank%d" % h) for h in range(ROW_TILES)]
        for h in range(ROW_TILES):
            cols = slice(h * P, (h + 1) * P)
            nc.tensor.matmul_mx(
                p_ps[h][:], lhsT=ws_w[:, cols].bitcast(E4M3X4), lhsT_scale=ws_plane[:, cols],
                rhs=x6_w[:].bitcast(E2M1X4), rhs_scale=x6_s[:], start=True, stop=False,
            )

        pairs = [slice(t, t + 2) for t in range(0, PACK, 2)]
        for pair in pairs:
            nc.vector.tensor_tensor(gated[:, pair, :], a_scaled[:, pair, :], gate[:, pair, :], ALU.mult)
        for pair in pairs:
            nc.vector.tensor_tensor(
                hid[:, :, pair], gated[:, pair, :].rearrange("p t o -> p o t"),
                b_scaled[:, pair, :].rearrange("p t o -> p o t"), ALU.subtract,
            )
        hid_w = sb_tile([P, O], U32, "hid_w")
        hid_s = sb_tile([P, O], U8, "hid_s")
        nc.vector.quantize_mx(out=hid_w[:].bitcast(E5M2X4), scales=hid_s[:], in_=hid[:].rearrange("p o t -> p (o t)"))
        for h in range(ROW_TILES):
            cols = slice(h * P, (h + 1) * P)
            nc.tensor.matmul_mx(
                p_ps[h][:], lhsT=wb_w[:, cols].bitcast(E2M1X4), lhsT_scale=wb_plane[:, cols],
                rhs=hid_w[:].bitcast(E5M2X4), rhs_scale=hid_s[:], start=False, stop=True,
            )

        p_sb = [sb_tile([P, O], F32, "p_sb%d" % h) for h in range(ROW_TILES)]
        nc.vector.tensor_copy(p_sb[0][:], p_ps[0][:])
        nc.scalar.copy(p_sb[1][:], p_ps[1][:])
        nc.vector.tensor_copy(pages[0][:].indirect(list7[:]), p_sb[0][:])
        nc.scalar.activation(pages[1][:].indirect(list7[:]), p_sb[1][:], ACT.Copy)
        nc.sync.dma_start(out[0:P, :], pages[0][:])
        nc.scalar.dma_start(out[P : 2 * P, :], pages[1][:])
